import numpy as np
import ml_dtypes


def mxq(x, axis, fmt="e4m3"):
    dtype, down = {"e4m3": (ml_dtypes.float8_e4m3fn, 7), "e5m2": (ml_dtypes.float8_e5m2, 14)}[fmt]
    v = np.moveaxis(np.asarray(x, np.float32).astype(ml_dtypes.bfloat16).astype(np.float64), axis, -1)
    blocks = v.reshape(v.shape[:-1] + (-1, 32))
    amax = np.abs(blocks).max(-1, keepdims=True)
    byte = np.maximum(np.where(amax > 0, np.frexp(amax)[1] - 1 + 127, 0) - down, 1)
    scale = np.exp2(byte - 127.0)
    codes = (blocks / scale).astype(np.float32).astype(dtype).astype(np.float64)
    return np.moveaxis((codes * scale).reshape(v.shape), -1, axis)


WIDE = False


def mx_kscale(k):
    if not WIDE:
        return np.ones(k)
    levels = np.array([10, -10, 5, -5, 0])
    if k % 512:
        return np.exp2(np.random.permutation(np.resize(levels, k // 32))).repeat(32)
    a = np.empty((k // 512, 16))
    for p in range(k // 512):
        a[p, :8] = np.random.permutation(np.resize(levels, 8))
        for g in range(8):
            far = levels[np.abs(levels - a[p, g]) >= 10]
            a[p, g + 8] = far[np.random.randint(len(far))]
    return np.exp2(a.ravel()).repeat(32)


def f64(x):
    return np.asarray(x).astype(np.float64)


def striped(idx):
    return np.tile(idx.reshape(-1, 16).T, (8, 1)).astype(np.uint16)


def unstriped(offs):
    return offs[:16].T.reshape(-1).astype(np.int64)


E2M1 = np.array([0.0, 0.5, 1.0, 1.5, 2.0, 3.0, 4.0, 6.0, -0.0, -0.5, -1.0, -1.5, -2.0, -3.0, -4.0, -6.0])


def pack_weight(w, fmt):
    k, n = w.shape
    w = f64(np.asarray(w, np.float32).astype(ml_dtypes.bfloat16)).reshape(k // 32, 32, n)
    amax = np.abs(w).max(1)
    if fmt == "e4m3":
        byte = np.frexp(amax)[1] - 1 + 127 - 7
    else:
        mant, ex = np.frexp(amax / 6.0)
        byte = np.where(mant > 0.5, ex, ex - 1) + 127
    byte = np.clip(np.where(amax > 0, byte, 1), 1, 254)
    scaled = (w * np.exp2(127.0 - byte)[:, None, :]).reshape(k, n).astype(np.float32)
    by_word = np.ascontiguousarray(scaled.reshape(k // 512, 128, 4, n).transpose(0, 1, 3, 2))
    if fmt == "e4m3":
        words = by_word.astype(ml_dtypes.float8_e4m3fn).view(np.uint8)
    else:
        c = by_word.astype(ml_dtypes.float4_e2m1fn).view(np.uint8) & 0xF
        words = (c[..., 0::2] | (c[..., 1::2] << 4)).reshape(k // 512, 128, 2 * n)
    return np.ascontiguousarray(words), np.ascontiguousarray(byte.astype(np.uint8).reshape(k // 512, 16, n))


def unpack_weight(words, scales, fmt):
    g, _, n = scales.shape
    words = np.ascontiguousarray(words).reshape(g, 128, n, -1)
    if fmt == "e4m3":
        vals = words.view(ml_dtypes.float8_e4m3fn).astype(np.float64)
    else:
        nib = np.empty((g, 128, n, 4), np.uint8)
        nib[..., 0::2] = words & 0xF
        nib[..., 1::2] = words >> 4
        vals = E2M1[nib]
    vals = vals * np.repeat(np.exp2(scales.astype(np.float64) - 127.0), 8, axis=1)[..., None]
    return vals.transpose(0, 1, 3, 2).reshape(g * 512, n)


def gelu(v):
    return 0.5 * v * (1.0 + np.tanh(np.sqrt(2.0 / np.pi) * (v + 0.044715 * v**3)))


K, KA, KB, H, T, S, P = 1536, 1024, 512, 1024, 4096, 1024, 512

def setup_inputs():
    n = np.random.standard_normal
    s = mx_kscale(K)[:, None]
    u = mx_kscale(H)[:, None]
    tab_words, tab_scales = pack_weight(n((K, T)) * s, "e4m3")
    w4_words, w4_scales = pack_weight(1.3 * n((KA, H)) / np.sqrt(K) / s[:KA], "e2m1")
    w1 = 1.3 * n((KB, H)) / np.sqrt(K) / s[KA:]
    return {
        "tab_words": tab_words, "tab_scales": tab_scales,
        "offs": striped(np.random.permutation(T)[:S]),
        "pos1": striped(np.random.permutation(S)[:P]),
        "pos2": striped(np.random.permutation(S)[:P]),
        "w4_words": w4_words, "w4_scales": w4_scales,
        "w1": w1.astype(np.float32),
        "force": np.exp(0.4 * n((H, S))).astype(np.float32),
        "gain": (np.exp(0.3 * n(H)) * u[:, 0]).astype(np.float32),
        "d": (1.4 * np.exp(0.3 * n(H)) / np.sqrt(H) / u[:, 0] ** 2).astype(np.float32),
        "base": (0.6 * n(P) - 0.3).astype(np.float32),
    }

def reference(tab_words, tab_scales, offs, pos1, pos2, w4_words, w4_scales, w1, force, gain, d, base):
    v = unpack_weight(tab_words, tab_scales, "e4m3")[:, unstriped(offs)]
    w4 = unpack_weight(w4_words, w4_scales, "e2m1")
    w1q = mxq(f64(w1), 0, "e4m3")
    h = np.tanh(w4.T @ v[:KA] + w1q.T @ v[KA:])
    h = h * f64(force) * f64(gain)[:, None]
    x1 = mxq(h[:, unstriped(pos1)], 0, "e4m3")
    x2 = mxq(np.abs(h[:, unstriped(pos2)]) * f64(d)[:, None], 0, "e4m3")
    e = x1.T @ x2
    return np.tanh(np.maximum(e, f64(base)[None, :]))

@@ -1,0 +1,267 @@
+from contextlib import ExitStack
+
+import concourse.mybir as mybir
+
+K, KA, KB, H, T, S, NP = 1536, 1024, 512, 1024, 4096, 1024, 512
+FLOPS = 2 * K * H * S + 2 * H * NP * NP
+
+F32 = mybir.dt.float32
+BF16 = mybir.dt.bfloat16
+I32 = mybir.dt.int32
+U32 = mybir.dt.uint32
+U16 = mybir.dt.uint16
+U8 = mybir.dt.uint8
+FP8X4 = mybir.dt.float8_e4m3fn_x4
+FP4X4 = mybir.dt.float4_e2m1fn_x4
+ALU = mybir.AluOpType
+ACT = mybir.ActivationFunctionType
+
+P = 128
+PACK = 4
+PASS = P * PACK
+BANK = 512
+QUADS = 4
+R_PASSES = H // PASS
+M_TILES = NP // P
+
+
+def interleave(copy, words, planes):
+    copy(
+        words.rearrange("p (c i t) -> p c t i", i=4, t=PACK),
+        planes.rearrange("p t (c i) -> p c t i", i=4),
+    )
+
+
+def tile_list_statute_reference_finder_kernel(
+    tc, tab_words, tab_scales, offs, pos1, pos2, w4_words, w4_scales, w1, force, gain, d, base, out
+):
+    nc = tc.nc
+    with ExitStack() as ctx:
+        keep = ctx.enter_context(tc.tile_pool(name="keep", bufs=1))
+        ring = ctx.enter_context(tc.tile_pool(name="ring", bufs=2))
+        h_psum = ctx.enter_context(tc.psum_pool(name="h_psum", bufs=4))
+        e_psum = ctx.enter_context(tc.psum_pool(name="e_psum", bufs=1))
+
+        offs_sb = keep.tile([P, S // 16], U16, name="offs_sb")
+        pos1_sb = keep.tile([P, NP // 16], U16, name="pos1_sb")
+        pos2_sb = keep.tile([P, NP // 16], U16, name="pos2_sb")
+        table = [keep.tile([P, T], U32, name="table%d" % a, align_bytes=64) for a in range(3)]
+        table_scale = keep.tile([P, T], U8, name="table_scale", align_bytes=64)
+        w4_raw = keep.tile([P, 2, 2 * H], U8, name="w4_raw", align_bytes=64)
+        w4_scale_raw = keep.tile([P, 2, H], U8, name="w4_scale_raw", align_bytes=64)
+        w1_raw = [keep.tile([P, PACK, PASS], F32, name="w1_raw%d" % b, align_bytes=64) for b in range(R_PASSES)]
+        force_sb = [keep.tile([P, S], F32, name="force%d" % s, align_bytes=64) for s in range(8)]
+        gain_sb = keep.tile([P, R_PASSES, PACK], F32, name="gain_sb")
+        d_sb = keep.tile([P, R_PASSES, PACK], F32, name="d_sb")
+        base_sb = keep.tile([P, NP], F32, name="base_sb", align_bytes=64)
+        v_scale1 = keep.tile([P, S], U8, name="v_scale1", align_bytes=64)
+
+        nc.vector.memset(table_scale[:].bitcast(I32), 0)
+        nc.vector.memset(w4_scale_raw[:].bitcast(I32), 0)
+        nc.vector.memset(v_scale1[:].bitcast(I32), 0)
+
+        def load_table(a):
+            nc.sync.dma_start(table[a][:].bitcast(I32), tab_words[a].rearrange("p t i -> p (t i)").bitcast(I32))
+
+        def load_w1(b):
+            nc.sync.dma_start(w1_raw[b][:], w1[:, b * PASS : (b + 1) * PASS].rearrange("(p j) c -> p j c", j=PACK))
+
+        force_rows = force.rearrange("(b p t) j -> b t p j", p=P, t=PACK)
+
+        def load_force(s):
+            nc.sync.dma_start(force_sb[s][:], force_rows[s // PACK, s % PACK])
+
+        nc.sync.dma_start(offs_sb[:], offs)
+        nc.sync.dma_start(w4_raw[:].bitcast(I32), w4_words.rearrange("a p c -> p a c").bitcast(I32))
+        for q in range(QUADS):
+            nc.gpsimd.dma_start(
+                table_scale[32 * q : 32 * q + 12, :].bitcast(I32), tab_scales[:, 4 * q : 4 * q + 4, :].bitcast(I32)
+            )
+        for q in range(QUADS):
+            nc.gpsimd.dma_start(
+                w4_scale_raw[32 * q : 32 * q + 4, :, :].bitcast(I32),
+                w4_scales[:, 4 * q : 4 * q + 4, :].rearrange("a r c -> r a c").bitcast(I32),
+            )
+        nc.scalar.dma_start(gain_sb[:], gain.rearrange("(b p t) -> p b t", p=P, t=PACK))
+        nc.scalar.dma_start(d_sb[:], d.rearrange("(b p t) -> p b t", p=P, t=PACK))
+        load_table(0)
+        load_table(1)
+        load_w1(0)
+        load_table(2)
+        load_force(0)
+        nc.sync.dma_start(pos2_sb[:], pos2)
+        nc.sync.dma_start(pos1_sb[:], pos1)
+        load_force(1)
+        load_force(2)
+        load_w1(1)
+        for s in range(3, 8):
+            load_force(s)
+        nc.sync.dma_start(base_sb[:], base.partition_broadcast(P))
+
+        w4_codes = keep.tile([P, 2, 2 * H], U8, name="w4_codes", align_bytes=64)
+        w4_scale = keep.tile([P, 2, H], U8, name="w4_scale", align_bytes=64)
+        for a in range(2):
+            nc.vector.tensor_copy(
+                w4_codes[:, a, :].bitcast(U16).rearrange("p (b t m) -> p b m t", b=R_PASSES, t=PACK),
+                w4_raw[:, a, :].bitcast(U16).rearrange("p (b m t) -> p b m t", b=R_PASSES, t=PACK),
+            )
+
+        two_or_zero = keep.tile([P, R_PASSES * PACK], F32, name="two_or_zero")
+        signed_gain = keep.tile([P, R_PASSES * PACK], F32, name="signed_gain")
+        d_cols = d_sb[:].rearrange("p b t -> p (b t)")
+        nc.vector.tensor_scalar(two_or_zero[:], d_cols, 0.0, 2.0, ALU.is_ge, ALU.mult)
+        nc.vector.scalar_tensor_tensor(
+            signed_gain[:], two_or_zero[:], -1.0, gain_sb[:].rearrange("p b t -> p (b t)"), ALU.add, ALU.mult
+        )
+
+        v_scale = keep.tile([P, S], U8, name="v_scale", align_bytes=64)
+        nc.vector.tensor_copy(v_scale[:], table_scale[:].indirect(offs_sb[:]))
+        for q in range(QUADS):
+            nc.gpsimd.dma_start(
+                v_scale1[32 * q : 32 * q + 4, :].bitcast(I32), v_scale[32 * q + 4 : 32 * q + 8, :].bitcast(I32)
+            )
+        v_words = [keep.tile([P, S], U32, name="v_words%d" % a, align_bytes=64) for a in range(3)]
+        nc.vector.tensor_copy(v_words[0][:], table[0][:].indirect(offs_sb[:]))
+        nc.vector.tensor_copy(
+            w4_scale[:].rearrange("p a c -> p (a c)").rearrange("p (g t m) -> p g m t", m=P, t=PACK),
+            w4_scale_raw[:].rearrange("p a c -> p (a c)").rearrange("p (g m t) -> p g m t", m=P, t=PACK),
+        )
+        nc.vector.tensor_copy(v_words[1][:], table[1][:].indirect(offs_sb[:]))
+
+        w1_codes = [keep.tile([P, PASS], U32, name="w1_codes%d" % b, align_bytes=64) for b in range(R_PASSES)]
+        w1_scale = [keep.tile([P, PASS], U8, name="w1_scale%d" % b, align_bytes=64) for b in range(R_PASSES)]
+
+        def quantize_w1(b):
+            grouped = ring.tile([P, PASS * PACK], BF16, name="w1_grouped", align_bytes=64)
+            nc.scalar.copy(
+                grouped[:].rearrange("p (t m j) -> p m j t", t=PACK, j=PACK),
+                w1_raw[b][:].rearrange("p j (m t) -> p m j t", t=PACK),
+            )
+            nc.vector.quantize_mx(out=w1_codes[b][:].bitcast(FP8X4), scales=w1_scale[b][:], in_=grouped[:])
+
+        quantize_w1(0)
+        for half in range(2):
+            nc.vector.tensor_copy(
+                v_words[2][:, half * BANK : (half + 1) * BANK],
+                table[2][:].indirect(offs_sb[:, half * 32 : (half + 1) * 32]),
+            )
+
+        def project(s):
+            b, t = divmod(s, PACK)
+            h = ring.tile([P, S], F32, name="h", align_bytes=64, bufs=6)
+            for half in range(2):
+                cols = slice(half * BANK, (half + 1) * BANK)
+                acc = h_psum.tile([P, BANK], F32, name="h_acc")
+                for a in range(2):
+                    nc.tensor.matmul_mx(
+                        out=acc[:],
+                        lhsT=w4_codes[:, a, 2 * P * s : 2 * P * (s + 1)].bitcast(FP4X4),
+                        lhsT_scale=w4_scale[:, a, P * s : P * (s + 1)],
+                        rhs=v_words[a][:, cols].bitcast(FP8X4),
+                        rhs_scale=(v_scale, v_scale1)[a][:, cols],
+                        start=(a == 0),
+                        stop=False,
+                    )
+                nc.tensor.matmul_mx(
+                    out=acc[:],
+                    lhsT=w1_codes[b][:, P * t : P * (t + 1)].bitcast(FP8X4),
+                    lhsT_scale=w1_scale[b][:, P * t : P * (t + 1)],
+                    rhs=v_words[2][:, cols].bitcast(FP8X4),
+                    rhs_scale=v_scale[8:P, cols],
+                    start=False,
+                    stop=True,
+                )
+                nc.scalar.activation(h[:, cols], acc[:], ACT.Tanh)
+            return h
+
+        def weigh(h, s, cols):
+            nc.vector.scalar_tensor_tensor(
+                h[:, cols], h[:, cols], signed_gain[:, s : s + 1], force_sb[s][:, cols], ALU.mult, ALU.mult
+            )
+
+        def pick_x2(h, s, planes):
+            picked = ring.tile([P, NP], F32, name="picked2", align_bytes=64, bufs=3)
+            nc.vector.tensor_copy(picked[:], h[:].indirect(pos2_sb[:]))
+            nc.scalar.activation(planes[:, s % PACK, :], picked[:], ACT.Abs, scale=d_cols[:, s : s + 1])
+
+        def pick_x1(h, s, planes, m0, m1):
+            nc.vector.tensor_copy(
+                planes[:, s % PACK, m0 * P : m1 * P], h[:].indirect(pos1_sb[:, 8 * m0 : 8 * m1])
+            )
+
+        def weave(copy, words, planes, m):
+            interleave(copy, words[:, m * PASS : (m + 1) * PASS], planes[:, :, m * P : (m + 1) * P])
+
+        e_acc = [e_psum.tile([P, NP], F32, name="e_acc%d" % m) for m in range(M_TILES)]
+        x1_planes = [keep.tile([P, PACK, NP], BF16, name="x1_planes%d" % b, align_bytes=64) for b in range(2)]
+        x2_planes = [keep.tile([P, PACK, NP], BF16, name="x2_planes%d" % b, align_bytes=64) for b in range(2)]
+        x1_words = [keep.tile([P, PACK * NP], BF16, name="x1_words%d" % b, align_bytes=64) for b in range(2)]
+        x2_words = [keep.tile([P, PACK * NP], BF16, name="x2_words%d" % b, align_bytes=64) for b in range(2)]
+        x1_codes = [keep.tile([P, NP], U32, name="x1_codes%d" % b, align_bytes=64) for b in range(2)]
+        x2_codes = [keep.tile([P, NP], U32, name="x2_codes%d" % b, align_bytes=64) for b in range(2)]
+        x1_scale = [keep.tile([P, NP], U8, name="x1_scale%d" % b, align_bytes=64) for b in range(2)]
+        x2_scale = [keep.tile([P, NP], U8, name="x2_scale%d" % b, align_bytes=64) for b in range(2)]
+
+        def quantize(codes, scale, words, m0, m1):
+            nc.vector.quantize_mx(
+                out=codes[:, m0 * P : m1 * P].bitcast(FP8X4),
+                scales=scale[:, m0 * P : m1 * P],
+                in_=words[:, m0 * PASS : m1 * PASS],
+            )
+
+        def score(m, b):
+            nc.tensor.matmul_mx(
+                out=e_acc[m][:],
+                lhsT=x1_codes[b][:, m * P : (m + 1) * P].bitcast(FP8X4),
+                lhsT_scale=x1_scale[b][:, m * P : (m + 1) * P],
+                rhs=x2_codes[b][:].bitcast(FP8X4),
+                rhs_scale=x2_scale[b][:],
+                start=(b == 0),
+                stop=(b == R_PASSES - 1),
+            )
+
+        def finish(m):
+            floored = ring.tile([P, NP], F32, name="floored", align_bytes=64)
+            nc.vector.tensor_tensor(floored[:], e_acc[m][:], base_sb[:], ALU.max)
+            result = ring.tile([P, NP], F32, name="result", align_bytes=64)
+            nc.scalar.activation(result[:], floored[:], ACT.Tanh)
+            nc.sync.dma_start(out[m * P : (m + 1) * P, :], result[:])
+
+        hs = [project(0), project(1)]
+        weigh(hs[0], 0, slice(0, BANK))
+        weigh(hs[0], 0, slice(BANK, S))
+        for s in range(8):
+            b = s // PACK
+            if s + 2 < 8:
+                hs.append(project(s + 2))
+            if s == 0:
+                quantize_w1(1)
+            if s + 1 < 8:
+                weigh(hs[s + 1], s + 1, slice(0, S))
+            pick_x2(hs[s], s, x2_planes[b])
+            if s <= PACK:
+                pick_x1(hs[s], s, x1_planes[b], 0, M_TILES)
+            if s in (4, 5):
+                planes, words = ((x1_planes, x1_words), (x2_planes, x2_words))[s - 4]
+                for m in range(M_TILES):
+                    weave(nc.scalar.copy, words[0], planes[0], m)
+            if s == 5:
+                quantize(x1_codes[0], x1_scale[0], x1_words[0], 0, M_TILES)
+            if s == 6:
+                quantize(x2_codes[0], x2_scale[0], x2_words[0], 0, M_TILES)
+                for m in range(M_TILES):
+                    score(m, 0)
+        for m in range(M_TILES):
+            weave(nc.scalar.copy, x2_words[1], x2_planes[1], m)
+        for m in range(M_TILES):
+            for s in range(5, 8):
+                pick_x1(hs[s], s, x1_planes[1], m, m + 1)
+            weave(nc.vector.tensor_copy if m == 0 else nc.scalar.copy, x1_words[1], x1_planes[1], m)
+            if m == 2:
+                quantize(x2_codes[1], x2_scale[1], x2_words[1], 0, M_TILES)
+        for m in range(M_TILES):
+            quantize(x1_codes[1], x1_scale[1], x1_words[1], m, m + 1)
+            score(m, 1)
+            if m > 0:
+                finish(m - 1)
+        finish(M_TILES - 1)

@@ -39,26 +39,24 @@ def tile_list_statute_reference_finder_kernel(
     with ExitStack() as ctx:
         keep = ctx.enter_context(tc.tile_pool(name="keep", bufs=1))
         ring = ctx.enter_context(tc.tile_pool(name="ring", bufs=2))
-        h_psum = ctx.enter_context(tc.psum_pool(name="h_psum", bufs=4))
-        e_psum = ctx.enter_context(tc.psum_pool(name="e_psum", bufs=1))
+        psum = ctx.enter_context(tc.psum_pool(name="psum", bufs=8))
 
         offs_sb = keep.tile([P, S // 16], U16, name="offs_sb")
         pos1_sb = keep.tile([P, NP // 16], U16, name="pos1_sb")
         pos2_sb = keep.tile([P, NP // 16], U16, name="pos2_sb")
         table = [keep.tile([P, T], U32, name="table%d" % a, align_bytes=64) for a in range(3)]
-        table_scale = keep.tile([P, T], U8, name="table_scale", align_bytes=64)
+        table_scale = [keep.tile([P, T], U8, name="table_scale%d" % i, align_bytes=64) for i in range(2)]
         w4_raw = keep.tile([P, 2, 2 * H], U8, name="w4_raw", align_bytes=64)
         w4_scale_raw = keep.tile([P, 2, H], U8, name="w4_scale_raw", align_bytes=64)
         w1_raw = [keep.tile([P, PACK, PASS], F32, name="w1_raw%d" % b, align_bytes=64) for b in range(R_PASSES)]
-        force_sb = [keep.tile([P, S], F32, name="force%d" % s, align_bytes=64) for s in range(8)]
+        force_sb = [keep.tile([P, S], F32, name="force%d" % s, tag="force%d" % s, align_bytes=64) for s in range(8)]
         gain_sb = keep.tile([P, R_PASSES, PACK], F32, name="gain_sb")
         d_sb = keep.tile([P, R_PASSES, PACK], F32, name="d_sb")
         base_sb = keep.tile([P, NP], F32, name="base_sb", align_bytes=64)
-        v_scale1 = keep.tile([P, S], U8, name="v_scale1", align_bytes=64)
 
-        nc.vector.memset(table_scale[:].bitcast(I32), 0)
         nc.vector.memset(w4_scale_raw[:].bitcast(I32), 0)
-        nc.vector.memset(v_scale1[:].bitcast(I32), 0)
+        nc.vector.memset(table_scale[0][:].bitcast(I32), 0)
+        nc.vector.memset(table_scale[1][:].bitcast(I32), 0)
 
         def load_table(a):
             nc.sync.dma_start(table[a][:].bitcast(I32), tab_words[a].rearrange("p t i -> p (t i)").bitcast(I32))
@@ -71,30 +69,31 @@ def tile_list_statute_reference_finder_kernel(
         def load_force(s):
             nc.sync.dma_start(force_sb[s][:], force_rows[s // PACK, s % PACK])
 
+        def load_table_scale(a, tile, row):
+            for r in range(4):
+                nc.sync.dma_start(tile[row + r : P : 32, :].bitcast(I32), tab_scales[a, r:16:4, :].bitcast(I32))
+
         nc.sync.dma_start(offs_sb[:], offs)
         nc.sync.dma_start(w4_raw[:].bitcast(I32), w4_words.rearrange("a p c -> p a c").bitcast(I32))
-        for q in range(QUADS):
-            nc.gpsimd.dma_start(
-                table_scale[32 * q : 32 * q + 12, :].bitcast(I32), tab_scales[:, 4 * q : 4 * q + 4, :].bitcast(I32)
+        for r in range(4):
+            nc.sync.dma_start(
+                w4_scale_raw[r:P:32, :, :].bitcast(I32),
+                w4_scales[:, r:16:4, :].rearrange("a q c -> q a c").bitcast(I32),
             )
-        for q in range(QUADS):
-            nc.gpsimd.dma_start(
-                w4_scale_raw[32 * q : 32 * q + 4, :, :].bitcast(I32),
-                w4_scales[:, 4 * q : 4 * q + 4, :].rearrange("a r c -> r a c").bitcast(I32),
-            )
-        nc.scalar.dma_start(gain_sb[:], gain.rearrange("(b p t) -> p b t", p=P, t=PACK))
-        nc.scalar.dma_start(d_sb[:], d.rearrange("(b p t) -> p b t", p=P, t=PACK))
+        load_table_scale(0, table_scale[0], 0)
+        load_table_scale(2, table_scale[0], 4)
+        load_table_scale(1, table_scale[1], 0)
         load_table(0)
         load_table(1)
         load_w1(0)
         load_table(2)
+        load_w1(1)
+        nc.sync.dma_start(gain_sb[:], gain.rearrange("(b p t) -> p b t", p=P, t=PACK))
+        nc.sync.dma_start(d_sb[:], d.rearrange("(b p t) -> p b t", p=P, t=PACK))
         load_force(0)
         nc.sync.dma_start(pos2_sb[:], pos2)
         nc.sync.dma_start(pos1_sb[:], pos1)
-        load_force(1)
-        load_force(2)
-        load_w1(1)
-        for s in range(3, 8):
+        for s in range(1, 8):
             load_force(s)
         nc.sync.dma_start(base_sb[:], base.partition_broadcast(P))
 
@@ -106,6 +105,39 @@ def tile_list_statute_reference_finder_kernel(
                 w4_raw[:, a, :].bitcast(U16).rearrange("p (b m t) -> p b m t", b=R_PASSES, t=PACK),
             )
 
+        nc.vector.tensor_copy(
+            w4_scale[:].rearrange("p a c -> p (a c)").rearrange("p (g t m) -> p g m t", m=P, t=PACK),
+            w4_scale_raw[:].rearrange("p a c -> p (a c)").rearrange("p (g m t) -> p g m t", m=P, t=PACK),
+        )
+        v_scale = [keep.tile([P, S], U8, name="v_scale%d" % i, align_bytes=64) for i in range(2)]
+        v_words = [keep.tile([P, S], U32, name="v_words%d" % a, align_bytes=64) for a in range(3)]
+        for i in range(2):
+            nc.vector.tensor_copy(v_scale[i][:], table_scale[i][:].indirect(offs_sb[:]))
+        for a in range(2):
+            nc.vector.tensor_copy(v_words[a][:], table[a][:].indirect(offs_sb[:]))
+
+        w1_codes = [keep.tile([P, PASS], U32, name="w1_codes%d" % b, align_bytes=64) for b in range(R_PASSES)]
+        w1_scale = [keep.tile([P, PASS], U8, name="w1_scale%d" % b, align_bytes=64) for b in range(R_PASSES)]
+
+        w1_grouped = [keep.tile([P, PASS * PACK], BF16, name="w1_grouped%d" % b, align_bytes=64) for b in range(2)]
+
+        def group_w1(copy, b):
+            copy(
+                w1_grouped[b][:].rearrange("p (t m j) -> p m j t", t=PACK, j=PACK),
+                w1_raw[b][:].rearrange("p j (m t) -> p m j t", t=PACK),
+            )
+
+        def quantize_w1(b):
+            nc.vector.quantize_mx(out=w1_codes[b][:].bitcast(FP8X4), scales=w1_scale[b][:], in_=w1_grouped[b][:])
+
+        group_w1(nc.scalar.copy, 0)
+        quantize_w1(0)
+        for half in range(2):
+            nc.vector.tensor_copy(
+                v_words[2][:, half * BANK : (half + 1) * BANK],
+                table[2][:].indirect(offs_sb[:, half * 32 : (half + 1) * 32]),
+            )
+
         two_or_zero = keep.tile([P, R_PASSES * PACK], F32, name="two_or_zero")
         signed_gain = keep.tile([P, R_PASSES * PACK], F32, name="signed_gain")
         d_cols = d_sb[:].rearrange("p b t -> p (b t)")
@@ -114,51 +146,22 @@ def tile_list_statute_reference_finder_kernel(
             signed_gain[:], two_or_zero[:], -1.0, gain_sb[:].rearrange("p b t -> p (b t)"), ALU.add, ALU.mult
         )
 
-        v_scale = keep.tile([P, S], U8, name="v_scale", align_bytes=64)
-        nc.vector.tensor_copy(v_scale[:], table_scale[:].indirect(offs_sb[:]))
-        for q in range(QUADS):
-            nc.gpsimd.dma_start(
-                v_scale1[32 * q : 32 * q + 4, :].bitcast(I32), v_scale[32 * q + 4 : 32 * q + 8, :].bitcast(I32)
-            )
-        v_words = [keep.tile([P, S], U32, name="v_words%d" % a, align_bytes=64) for a in range(3)]
-        nc.vector.tensor_copy(v_words[0][:], table[0][:].indirect(offs_sb[:]))
-        nc.vector.tensor_copy(
-            w4_scale[:].rearrange("p a c -> p (a c)").rearrange("p (g t m) -> p g m t", m=P, t=PACK),
-            w4_scale_raw[:].rearrange("p a c -> p (a c)").rearrange("p (g m t) -> p g m t", m=P, t=PACK),
-        )
-        nc.vector.tensor_copy(v_words[1][:], table[1][:].indirect(offs_sb[:]))
-
-        w1_codes = [keep.tile([P, PASS], U32, name="w1_codes%d" % b, align_bytes=64) for b in range(R_PASSES)]
-        w1_scale = [keep.tile([P, PASS], U8, name="w1_scale%d" % b, align_bytes=64) for b in range(R_PASSES)]
-
-        def quantize_w1(b):
-            grouped = ring.tile([P, PASS * PACK], BF16, name="w1_grouped", align_bytes=64)
-            nc.scalar.copy(
-                grouped[:].rearrange("p (t m j) -> p m j t", t=PACK, j=PACK),
-                w1_raw[b][:].rearrange("p j (m t) -> p m j t", t=PACK),
-            )
-            nc.vector.quantize_mx(out=w1_codes[b][:].bitcast(FP8X4), scales=w1_scale[b][:], in_=grouped[:])
-
-        quantize_w1(0)
-        for half in range(2):
-            nc.vector.tensor_copy(
-                v_words[2][:, half * BANK : (half + 1) * BANK],
-                table[2][:].indirect(offs_sb[:, half * 32 : (half + 1) * 32]),
-            )
+        gain_d = keep.tile([P, R_PASSES * PACK], F32, name="gain_d")
+        nc.vector.tensor_tensor(gain_d[:], gain_sb[:].rearrange("p b t -> p (b t)"), d_cols, ALU.mult)
 
         def project(s):
             b, t = divmod(s, PACK)
             h = ring.tile([P, S], F32, name="h", align_bytes=64, bufs=6)
             for half in range(2):
                 cols = slice(half * BANK, (half + 1) * BANK)
-                acc = h_psum.tile([P, BANK], F32, name="h_acc")
+                acc = psum.tile([P, BANK], F32, name="h_acc", tag="bank")
                 for a in range(2):
                     nc.tensor.matmul_mx(
                         out=acc[:],
                         lhsT=w4_codes[:, a, 2 * P * s : 2 * P * (s + 1)].bitcast(FP4X4),
                         lhsT_scale=w4_scale[:, a, P * s : P * (s + 1)],
                         rhs=v_words[a][:, cols].bitcast(FP8X4),
-                        rhs_scale=(v_scale, v_scale1)[a][:, cols],
+                        rhs_scale=v_scale[a][:, cols],
                         start=(a == 0),
                         stop=False,
                     )
@@ -167,38 +170,35 @@ def tile_list_statute_reference_finder_kernel(
                     lhsT=w1_codes[b][:, P * t : P * (t + 1)].bitcast(FP8X4),
                     lhsT_scale=w1_scale[b][:, P * t : P * (t + 1)],
                     rhs=v_words[2][:, cols].bitcast(FP8X4),
-                    rhs_scale=v_scale[8:P, cols],
+                    rhs_scale=v_scale[0][4:P, cols],
                     start=False,
                     stop=True,
                 )
                 nc.scalar.activation(h[:, cols], acc[:], ACT.Tanh)
             return h
 
-        def weigh(h, s, cols):
-            nc.vector.scalar_tensor_tensor(
-                h[:, cols], h[:, cols], signed_gain[:, s : s + 1], force_sb[s][:, cols], ALU.mult, ALU.mult
-            )
+        def weigh(engine, h, s, cols):
+            engine.tensor_tensor(h[:, cols], h[:, cols], force_sb[s][:, cols], ALU.mult)
 
         def pick_x2(h, s, planes):
             picked = ring.tile([P, NP], F32, name="picked2", align_bytes=64, bufs=3)
             nc.vector.tensor_copy(picked[:], h[:].indirect(pos2_sb[:]))
-            nc.scalar.activation(planes[:, s % PACK, :], picked[:], ACT.Abs, scale=d_cols[:, s : s + 1])
+            nc.scalar.activation(planes[:, s % PACK, :], picked[:], ACT.Abs, scale=gain_d[:, s : s + 1])
 
-        def pick_x1(h, s, planes, m0, m1):
-            nc.vector.tensor_copy(
-                planes[:, s % PACK, m0 * P : m1 * P], h[:].indirect(pos1_sb[:, 8 * m0 : 8 * m1])
-            )
+        def pick_x1(h, s, planes):
+            picked = ring.tile([P, NP], F32, name="picked1", align_bytes=64, bufs=3)
+            nc.vector.tensor_copy(picked[:], h[:].indirect(pos1_sb[:]))
+            nc.scalar.activation(planes[:, s % PACK, :], picked[:], ACT.Copy, scale=signed_gain[:, s : s + 1])
 
         def weave(copy, words, planes, m):
             interleave(copy, words[:, m * PASS : (m + 1) * PASS], planes[:, :, m * P : (m + 1) * P])
 
-        e_acc = [e_psum.tile([P, NP], F32, name="e_acc%d" % m) for m in range(M_TILES)]
+        e_acc = []
         x1_planes = [keep.tile([P, PACK, NP], BF16, name="x1_planes%d" % b, align_bytes=64) for b in range(2)]
         x2_planes = [keep.tile([P, PACK, NP], BF16, name="x2_planes%d" % b, align_bytes=64) for b in range(2)]
         x1_words = [keep.tile([P, PACK * NP], BF16, name="x1_words%d" % b, align_bytes=64) for b in range(2)]
         x2_words = [keep.tile([P, PACK * NP], BF16, name="x2_words%d" % b, align_bytes=64) for b in range(2)]
-        x1_codes = [keep.tile([P, NP], U32, name="x1_codes%d" % b, align_bytes=64) for b in range(2)]
-        x2_codes = [keep.tile([P, NP], U32, name="x2_codes%d" % b, align_bytes=64) for b in range(2)]
+        x1_codes, x2_codes = [], []
         x1_scale = [keep.tile([P, NP], U8, name="x1_scale%d" % b, align_bytes=64) for b in range(2)]
         x2_scale = [keep.tile([P, NP], U8, name="x2_scale%d" % b, align_bytes=64) for b in range(2)]
 
@@ -214,54 +214,63 @@ def tile_list_statute_reference_finder_kernel(
                 out=e_acc[m][:],
                 lhsT=x1_codes[b][:, m * P : (m + 1) * P].bitcast(FP8X4),
                 lhsT_scale=x1_scale[b][:, m * P : (m + 1) * P],
-                rhs=x2_codes[b][:].bitcast(FP8X4),
+                rhs=x2_codes[b][:, :].bitcast(FP8X4),
                 rhs_scale=x2_scale[b][:],
                 start=(b == 0),
                 stop=(b == R_PASSES - 1),
             )
 
-        def finish(m):
-            floored = ring.tile([P, NP], F32, name="floored", align_bytes=64)
-            nc.vector.tensor_tensor(floored[:], e_acc[m][:], base_sb[:], ALU.max)
-            result = ring.tile([P, NP], F32, name="result", align_bytes=64)
-            nc.scalar.activation(result[:], floored[:], ACT.Tanh)
-            nc.sync.dma_start(out[m * P : (m + 1) * P, :], result[:])
+        results = [keep.tile([P, NP], F32, name="result%d" % m, align_bytes=64) for m in range(M_TILES)]
 
-        hs = [project(0), project(1)]
-        weigh(hs[0], 0, slice(0, BANK))
-        weigh(hs[0], 0, slice(BANK, S))
+        def finish(m, cols):
+            nc.vector.tensor_tensor(results[m][:, cols], e_acc[m][:, cols], base_sb[:, cols], ALU.max)
+            nc.scalar.activation(results[m][:, cols], results[m][:, cols], ACT.Tanh)
+            nc.sync.dma_start(out[m * P : (m + 1) * P, cols], results[m][:, cols])
+
+        halves = (slice(0, BANK), slice(BANK, S))
+        hs = [project(0), project(1), project(2)]
+        group_w1(nc.vector.tensor_copy, 1)
+        for cols in halves:
+            weigh(nc.vector, hs[0], 0, cols)
+        quantize_w1(1)
+        for cols in halves:
+            weigh(nc.gpsimd, hs[1], 1, cols)
+        first_weaves = [(x2_words[0], x2_planes[0], m) for m in range(M_TILES)]
+        first_weaves.extend((x1_words[0], x1_planes[0], m) for m in range(M_TILES))
         for s in range(8):
             b = s // PACK
+            if s + 3 < 8:
+                hs.append(project(s + 3))
             if s + 2 < 8:
-                hs.append(project(s + 2))
-            if s == 0:
-                quantize_w1(1)
-            if s + 1 < 8:
-                weigh(hs[s + 1], s + 1, slice(0, S))
+                for cols in halves:
+                    weigh(nc.gpsimd, hs[s + 2], s + 2, cols)
             pick_x2(hs[s], s, x2_planes[b])
-            if s <= PACK:
-                pick_x1(hs[s], s, x1_planes[b], 0, M_TILES)
-            if s in (4, 5):
-                planes, words = ((x1_planes, x1_words), (x2_planes, x2_words))[s - 4]
-                for m in range(M_TILES):
-                    weave(nc.scalar.copy, words[0], planes[0], m)
-            if s == 5:
-                quantize(x1_codes[0], x1_scale[0], x1_words[0], 0, M_TILES)
+            pick_x1(hs[s], s, x1_planes[b])
+            if s in (3, 4, 5):
+                for job in first_weaves[3 * (s - 3) : 3 * (s - 2)]:
+                    weave(nc.scalar.copy, *job)
             if s == 6:
+                first_codes = keep.tile([P, 2, NP], U32, name="first_codes", tag="force7", align_bytes=64)
+                x1_codes.append(first_codes[:, 0, :])
+                x2_codes.append(first_codes[:, 1, :])
                 quantize(x2_codes[0], x2_scale[0], x2_words[0], 0, M_TILES)
+                quantize(x1_codes[0], x1_scale[0], x1_words[0], 0, M_TILES)
                 for m in range(M_TILES):
+                    e_acc.append(psum.tile([P, NP], F32, name="e_acc", tag="bank"))
                     score(m, 0)
+        x1_codes.append(keep.tile([P, NP], U32, name="x1_codes", align_bytes=64))
+        x2_codes.append(keep.tile([P, NP], U32, name="x2_codes", align_bytes=64))
         for m in range(M_TILES):
-            weave(nc.scalar.copy, x2_words[1], x2_planes[1], m)
-        for m in range(M_TILES):
-            for s in range(5, 8):
-                pick_x1(hs[s], s, x1_planes[1], m, m + 1)
-            weave(nc.vector.tensor_copy if m == 0 else nc.scalar.copy, x1_words[1], x1_planes[1], m)
-            if m == 2:
-                quantize(x2_codes[1], x2_scale[1], x2_words[1], 0, M_TILES)
-        for m in range(M_TILES):
-            quantize(x1_codes[1], x1_scale[1], x1_words[1], m, m + 1)
-            score(m, 1)
-            if m > 0:
-                finish(m - 1)
-        finish(M_TILES - 1)
+            weave(nc.vector.tensor_copy, x2_words[1], x2_planes[1], m)
+        for m in range(M_TILES - 1):
+            weave(nc.scalar.copy, x1_words[1], x1_planes[1], m)
+        quantize(x2_codes[1], x2_scale[1], x2_words[1], 0, M_TILES)
+        weave(nc.vector.tensor_copy, x1_words[1], x1_planes[1], M_TILES - 1)
+        for m0 in (0, 2):
+            quantize(x1_codes[1], x1_scale[1], x1_words[1], m0, m0 + 2)
+            score(m0, 1)
+            score(m0 + 1, 1)
+        for m in range(M_TILES - 1):
+            finish(m, slice(0, NP))
+        finish(M_TILES - 1, slice(0, NP // 2))
+        finish(M_TILES - 1, slice(NP // 2, NP))

from contextlib import ExitStack

import concourse.mybir as mybir

K, KA, KB, H, T, S, NP = 1536, 1024, 512, 1024, 4096, 1024, 512
FLOPS = 2 * K * H * S + 2 * H * NP * NP

F32 = mybir.dt.float32
BF16 = mybir.dt.bfloat16
I32 = mybir.dt.int32
U32 = mybir.dt.uint32
U16 = mybir.dt.uint16
U8 = mybir.dt.uint8
FP8X4 = mybir.dt.float8_e4m3fn_x4
FP4X4 = mybir.dt.float4_e2m1fn_x4
ALU = mybir.AluOpType
ACT = mybir.ActivationFunctionType

P = 128
PACK = 4
PASS = P * PACK
BANK = 512
QUADS = 4
R_PASSES = H // PASS
M_TILES = NP // P


def interleave(copy, words, planes):
    copy(
        words.rearrange("p (c i t) -> p c t i", i=4, t=PACK),
        planes.rearrange("p t (c i) -> p c t i", i=4),
    )


def tile_list_statute_reference_finder_kernel(
    tc, tab_words, tab_scales, offs, pos1, pos2, w4_words, w4_scales, w1, force, gain, d, base, out
):
    nc = tc.nc
    with ExitStack() as ctx:
        keep = ctx.enter_context(tc.tile_pool(name="keep", bufs=1))
        ring = ctx.enter_context(tc.tile_pool(name="ring", bufs=2))
        psum = ctx.enter_context(tc.psum_pool(name="psum", bufs=8))

        offs_sb = keep.tile([P, S // 16], U16, name="offs_sb")
        pos1_sb = keep.tile([P, NP // 16], U16, name="pos1_sb")
        pos2_sb = keep.tile([P, NP // 16], U16, name="pos2_sb")
        table = [keep.tile([P, T], U32, name="table%d" % a, align_bytes=64) for a in range(3)]
        table_scale = [keep.tile([P, T], U8, name="table_scale%d" % i, align_bytes=64) for i in range(2)]
        w4_raw = keep.tile([P, 2, 2 * H], U8, name="w4_raw", align_bytes=64)
        w4_scale_raw = keep.tile([P, 2, H], U8, name="w4_scale_raw", align_bytes=64)
        w1_raw = [keep.tile([P, PACK, PASS], F32, name="w1_raw%d" % b, align_bytes=64) for b in range(R_PASSES)]
        force_sb = [keep.tile([P, S], F32, name="force%d" % s, tag="force%d" % s, align_bytes=64) for s in range(8)]
        gain_sb = keep.tile([P, R_PASSES, PACK], F32, name="gain_sb")
        d_sb = keep.tile([P, R_PASSES, PACK], F32, name="d_sb")
        base_sb = keep.tile([P, NP], F32, name="base_sb", align_bytes=64)

        nc.vector.memset(w4_scale_raw[:].bitcast(I32), 0)
        nc.vector.memset(table_scale[0][:].bitcast(I32), 0)
        nc.vector.memset(table_scale[1][:].bitcast(I32), 0)

        def load_table(a):
            nc.sync.dma_start(table[a][:].bitcast(I32), tab_words[a].rearrange("p t i -> p (t i)").bitcast(I32))

        def load_w1(b):
            nc.sync.dma_start(w1_raw[b][:], w1[:, b * PASS : (b + 1) * PASS].rearrange("(p j) c -> p j c", j=PACK))

        force_rows = force.rearrange("(b p t) j -> b t p j", p=P, t=PACK)

        def load_force(s):
            nc.sync.dma_start(force_sb[s][:], force_rows[s // PACK, s % PACK])

        def load_table_scale(a, tile, row):
            for r in range(4):
                nc.sync.dma_start(tile[row + r : P : 32, :].bitcast(I32), tab_scales[a, r:16:4, :].bitcast(I32))

        nc.sync.dma_start(offs_sb[:], offs)
        nc.sync.dma_start(w4_raw[:].bitcast(I32), w4_words.rearrange("a p c -> p a c").bitcast(I32))
        for r in range(4):
            nc.sync.dma_start(
                w4_scale_raw[r:P:32, :, :].bitcast(I32),
                w4_scales[:, r:16:4, :].rearrange("a q c -> q a c").bitcast(I32),
            )
        load_table_scale(0, table_scale[0], 0)
        load_table_scale(2, table_scale[0], 4)
        load_table_scale(1, table_scale[1], 0)
        load_table(0)
        load_table(1)
        load_w1(0)
        load_table(2)
        load_w1(1)
        nc.sync.dma_start(gain_sb[:], gain.rearrange("(b p t) -> p b t", p=P, t=PACK))
        nc.sync.dma_start(d_sb[:], d.rearrange("(b p t) -> p b t", p=P, t=PACK))
        load_force(0)
        nc.sync.dma_start(pos2_sb[:], pos2)
        nc.sync.dma_start(pos1_sb[:], pos1)
        for s in range(1, 8):
            load_force(s)
        nc.sync.dma_start(base_sb[:], base.partition_broadcast(P))

        w4_codes = keep.tile([P, 2, 2 * H], U8, name="w4_codes", align_bytes=64)
        w4_scale = keep.tile([P, 2, H], U8, name="w4_scale", align_bytes=64)
        for a in range(2):
            nc.vector.tensor_copy(
                w4_codes[:, a, :].bitcast(U16).rearrange("p (b t m) -> p b m t", b=R_PASSES, t=PACK),
                w4_raw[:, a, :].bitcast(U16).rearrange("p (b m t) -> p b m t", b=R_PASSES, t=PACK),
            )

        nc.vector.tensor_copy(
            w4_scale[:].rearrange("p a c -> p (a c)").rearrange("p (g t m) -> p g m t", m=P, t=PACK),
            w4_scale_raw[:].rearrange("p a c -> p (a c)").rearrange("p (g m t) -> p g m t", m=P, t=PACK),
        )
        v_scale = [keep.tile([P, S], U8, name="v_scale%d" % i, align_bytes=64) for i in range(2)]
        v_words = [keep.tile([P, S], U32, name="v_words%d" % a, align_bytes=64) for a in range(3)]
        for i in range(2):
            nc.vector.tensor_copy(v_scale[i][:], table_scale[i][:].indirect(offs_sb[:]))
        for a in range(2):
            nc.vector.tensor_copy(v_words[a][:], table[a][:].indirect(offs_sb[:]))

        w1_codes = [keep.tile([P, PASS], U32, name="w1_codes%d" % b, align_bytes=64) for b in range(R_PASSES)]
        w1_scale = [keep.tile([P, PASS], U8, name="w1_scale%d" % b, align_bytes=64) for b in range(R_PASSES)]

        w1_grouped = [keep.tile([P, PASS * PACK], BF16, name="w1_grouped%d" % b, align_bytes=64) for b in range(2)]

        def group_w1(copy, b):
            copy(
                w1_grouped[b][:].rearrange("p (t m j) -> p m j t", t=PACK, j=PACK),
                w1_raw[b][:].rearrange("p j (m t) -> p m j t", t=PACK),
            )

        def quantize_w1(b):
            nc.vector.quantize_mx(out=w1_codes[b][:].bitcast(FP8X4), scales=w1_scale[b][:], in_=w1_grouped[b][:])

        group_w1(nc.scalar.copy, 0)
        quantize_w1(0)
        for half in range(2):
            nc.vector.tensor_copy(
                v_words[2][:, half * BANK : (half + 1) * BANK],
                table[2][:].indirect(offs_sb[:, half * 32 : (half + 1) * 32]),
            )

        two_or_zero = keep.tile([P, R_PASSES * PACK], F32, name="two_or_zero")
        signed_gain = keep.tile([P, R_PASSES * PACK], F32, name="signed_gain")
        d_cols = d_sb[:].rearrange("p b t -> p (b t)")
        nc.vector.tensor_scalar(two_or_zero[:], d_cols, 0.0, 2.0, ALU.is_ge, ALU.mult)
        nc.vector.scalar_tensor_tensor(
            signed_gain[:], two_or_zero[:], -1.0, gain_sb[:].rearrange("p b t -> p (b t)"), ALU.add, ALU.mult
        )

        gain_d = keep.tile([P, R_PASSES * PACK], F32, name="gain_d")
        nc.vector.tensor_tensor(gain_d[:], gain_sb[:].rearrange("p b t -> p (b t)"), d_cols, ALU.mult)

        def project(s):
            b, t = divmod(s, PACK)
            h = ring.tile([P, S], F32, name="h", align_bytes=64, bufs=6)
            for half in range(2):
                cols = slice(half * BANK, (half + 1) * BANK)
                acc = psum.tile([P, BANK], F32, name="h_acc", tag="bank")
                for a in range(2):
                    nc.tensor.matmul_mx(
                        out=acc[:],
                        lhsT=w4_codes[:, a, 2 * P * s : 2 * P * (s + 1)].bitcast(FP4X4),
                        lhsT_scale=w4_scale[:, a, P * s : P * (s + 1)],
                        rhs=v_words[a][:, cols].bitcast(FP8X4),
                        rhs_scale=v_scale[a][:, cols],
                        start=(a == 0),
                        stop=False,
                    )
                nc.tensor.matmul_mx(
                    out=acc[:],
                    lhsT=w1_codes[b][:, P * t : P * (t + 1)].bitcast(FP8X4),
                    lhsT_scale=w1_scale[b][:, P * t : P * (t + 1)],
                    rhs=v_words[2][:, cols].bitcast(FP8X4),
                    rhs_scale=v_scale[0][4:P, cols],
                    start=False,
                    stop=True,
                )
                nc.scalar.activation(h[:, cols], acc[:], ACT.Tanh)
            return h

        def weigh(engine, h, s, cols):
            engine.tensor_tensor(h[:, cols], h[:, cols], force_sb[s][:, cols], ALU.mult)

        def pick_x2(h, s, planes):
            picked = ring.tile([P, NP], F32, name="picked2", align_bytes=64, bufs=3)
            nc.vector.tensor_copy(picked[:], h[:].indirect(pos2_sb[:]))
            nc.scalar.activation(planes[:, s % PACK, :], picked[:], ACT.Abs, scale=gain_d[:, s : s + 1])

        def pick_x1(h, s, planes):
            picked = ring.tile([P, NP], F32, name="picked1", align_bytes=64, bufs=3)
            nc.vector.tensor_copy(picked[:], h[:].indirect(pos1_sb[:]))
            nc.scalar.activation(planes[:, s % PACK, :], picked[:], ACT.Copy, scale=signed_gain[:, s : s + 1])

        def weave(copy, words, planes, m):
            interleave(copy, words[:, m * PASS : (m + 1) * PASS], planes[:, :, m * P : (m + 1) * P])

        e_acc = []
        x1_planes = [keep.tile([P, PACK, NP], BF16, name="x1_planes%d" % b, align_bytes=64) for b in range(2)]
        x2_planes = [keep.tile([P, PACK, NP], BF16, name="x2_planes%d" % b, align_bytes=64) for b in range(2)]
        x1_words = [keep.tile([P, PACK * NP], BF16, name="x1_words%d" % b, align_bytes=64) for b in range(2)]
        x2_words = [keep.tile([P, PACK * NP], BF16, name="x2_words%d" % b, align_bytes=64) for b in range(2)]
        x1_codes, x2_codes = [], []
        x1_scale = [keep.tile([P, NP], U8, name="x1_scale%d" % b, align_bytes=64) for b in range(2)]
        x2_scale = [keep.tile([P, NP], U8, name="x2_scale%d" % b, align_bytes=64) for b in range(2)]

        def quantize(codes, scale, words, m0, m1):
            nc.vector.quantize_mx(
                out=codes[:, m0 * P : m1 * P].bitcast(FP8X4),
                scales=scale[:, m0 * P : m1 * P],
                in_=words[:, m0 * PASS : m1 * PASS],
            )

        def score(m, b):
            nc.tensor.matmul_mx(
                out=e_acc[m][:],
                lhsT=x1_codes[b][:, m * P : (m + 1) * P].bitcast(FP8X4),
                lhsT_scale=x1_scale[b][:, m * P : (m + 1) * P],
                rhs=x2_codes[b][:, :].bitcast(FP8X4),
                rhs_scale=x2_scale[b][:],
                start=(b == 0),
                stop=(b == R_PASSES - 1),
            )

        results = [keep.tile([P, NP], F32, name="result%d" % m, align_bytes=64) for m in range(M_TILES)]

        def finish(m, cols):
            nc.vector.tensor_tensor(results[m][:, cols], e_acc[m][:, cols], base_sb[:, cols], ALU.max)
            nc.scalar.activation(results[m][:, cols], results[m][:, cols], ACT.Tanh)
            nc.sync.dma_start(out[m * P : (m + 1) * P, cols], results[m][:, cols])

        halves = (slice(0, BANK), slice(BANK, S))
        hs = [project(0), project(1), project(2)]
        group_w1(nc.vector.tensor_copy, 1)
        for cols in halves:
            weigh(nc.vector, hs[0], 0, cols)
        quantize_w1(1)
        for cols in halves:
            weigh(nc.gpsimd, hs[1], 1, cols)
        first_weaves = [(x2_words[0], x2_planes[0], m) for m in range(M_TILES)]
        first_weaves.extend((x1_words[0], x1_planes[0], m) for m in range(M_TILES))
        for s in range(8):
            b = s // PACK
            if s + 3 < 8:
                hs.append(project(s + 3))
            if s + 2 < 8:
                for cols in halves:
                    weigh(nc.gpsimd, hs[s + 2], s + 2, cols)
            pick_x2(hs[s], s, x2_planes[b])
            pick_x1(hs[s], s, x1_planes[b])
            if s in (3, 4, 5):
                for job in first_weaves[3 * (s - 3) : 3 * (s - 2)]:
                    weave(nc.scalar.copy, *job)
            if s == 6:
                first_codes = keep.tile([P, 2, NP], U32, name="first_codes", tag="force7", align_bytes=64)
                x1_codes.append(first_codes[:, 0, :])
                x2_codes.append(first_codes[:, 1, :])
                quantize(x2_codes[0], x2_scale[0], x2_words[0], 0, M_TILES)
                quantize(x1_codes[0], x1_scale[0], x1_words[0], 0, M_TILES)
                for m in range(M_TILES):
                    e_acc.append(psum.tile([P, NP], F32, name="e_acc", tag="bank"))
                    score(m, 0)
        x1_codes.append(keep.tile([P, NP], U32, name="x1_codes", align_bytes=64))
        x2_codes.append(keep.tile([P, NP], U32, name="x2_codes", align_bytes=64))
        for m in range(M_TILES):
            weave(nc.vector.tensor_copy, x2_words[1], x2_planes[1], m)
        for m in range(M_TILES - 1):
            weave(nc.scalar.copy, x1_words[1], x1_planes[1], m)
        quantize(x2_codes[1], x2_scale[1], x2_words[1], 0, M_TILES)
        weave(nc.vector.tensor_copy, x1_words[1], x1_planes[1], M_TILES - 1)
        for m0 in (0, 2):
            quantize(x1_codes[1], x1_scale[1], x1_words[1], m0, m0 + 2)
            score(m0, 1)
            score(m0 + 1, 1)
        for m in range(M_TILES - 1):
            finish(m, slice(0, NP))
        finish(M_TILES - 1, slice(0, NP // 2))
        finish(M_TILES - 1, slice(NP // 2, NP))
